import numpy as np
import ml_dtypes


def mxq(x, axis, fmt="e4m3"):
    dtype, down = {"e4m3": (ml_dtypes.float8_e4m3fn, 7), "e5m2": (ml_dtypes.float8_e5m2, 14)}[fmt]
    v = np.moveaxis(np.asarray(x, np.float32).astype(ml_dtypes.bfloat16).astype(np.float64), axis, -1)
    blocks = v.reshape(v.shape[:-1] + (-1, 32))
    amax = np.abs(blocks).max(-1, keepdims=True)
    byte = np.maximum(np.where(amax > 0, np.frexp(amax)[1] - 1 + 127, 0) - down, 1)
    scale = np.exp2(byte - 127.0)
    codes = (blocks / scale).astype(np.float32).astype(dtype).astype(np.float64)
    return np.moveaxis((codes * scale).reshape(v.shape), -1, axis)


WIDE = False


def mx_kscale(k):
    if not WIDE:
        return np.ones(k)
    levels = np.array([10, -10, 5, -5, 0])
    if k % 512:
        return np.exp2(np.random.permutation(np.resize(levels, k // 32))).repeat(32)
    a = np.empty((k // 512, 16))
    for p in range(k // 512):
        a[p, :8] = np.random.permutation(np.resize(levels, 8))
        for g in range(8):
            far = levels[np.abs(levels - a[p, g]) >= 10]
            a[p, g + 8] = far[np.random.randint(len(far))]
    return np.exp2(a.ravel()).repeat(32)


def f64(x):
    return np.asarray(x).astype(np.float64)


def striped(idx):
    return np.tile(idx.reshape(-1, 16).T, (8, 1)).astype(np.uint16)


def unstriped(offs):
    return offs[:16].T.reshape(-1).astype(np.int64)


def striped8(idx):
    return np.concatenate([x.reshape(-1, 16).T for x in idx]).astype(np.uint16)


def runs(offs, k):
    lists = np.stack([offs[16 * r : 16 * r + 16].T.reshape(-1) for r in range(8)]).astype(np.int64)
    return lists[np.arange(k) % 512 // 64]


def pack_weight(w):
    k, n = w.shape
    w = f64(np.asarray(w, np.float32).astype(ml_dtypes.bfloat16)).reshape(k // 32, 32, n)
    amax = np.abs(w).max(1)
    byte = np.clip(np.where(amax > 0, np.frexp(amax)[1] - 1 + 127 - 7, 1), 1, 254)
    scaled = (w * np.exp2(127.0 - byte)[:, None, :]).reshape(k, n).astype(np.float32)
    words = np.ascontiguousarray(scaled.reshape(k // 512, 128, 4, n).transpose(0, 1, 3, 2)).astype(ml_dtypes.float8_e4m3fn).view(np.uint8)
    return words, np.ascontiguousarray(byte.astype(np.uint8).reshape(k // 512, 16, n))


def unpack_weight(words, scales):
    g, p, n, _ = words.shape
    vals = np.ascontiguousarray(words).view(ml_dtypes.float8_e4m3fn).astype(np.float64) * np.repeat(np.exp2(scales.astype(np.float64) - 127.0), 8, axis=1)[..., None]
    return vals.transpose(0, 1, 3, 2).reshape(g * 512, n)

def planes(y):
    n, m = y.shape
    v = y.astype(np.float32).astype(ml_dtypes.bfloat16).astype(np.float64).reshape(n // 32, 32, m)
    top = np.abs(v).max(1)
    byte = np.clip(np.where(top > 0, np.frexp(top)[1] - 1 + 127 - 7, 1), 1, 254)
    codes = (v * np.exp2(127.0 - byte)[:, None, :]).reshape(n, m).astype(np.float32).astype(ml_dtypes.float8_e4m3fn).view(np.uint8)
    words = codes.reshape(n // 512, 128, 4, m).transpose(0, 1, 3, 2)
    return np.ascontiguousarray(words), np.ascontiguousarray(byte.astype(np.uint8).reshape(n // 512, 16, m))


K, T, S, H, W = 512, 2048, 512, 512, 256


def setup_inputs():
    n = np.random.standard_normal
    s = mx_kscale(K)[:, None]
    u = mx_kscale(S)
    packed_xT = pack_weight(n((K, T)) * s)
    packed_w1 = pack_weight(n((K, H)) / np.sqrt(K) / s)
    perm = np.stack([np.random.permutation(S) for _ in range(8)])
    return {
        "x_words": packed_xT[0],
        "x_scales": packed_xT[1],
        "w1_words": packed_w1[0],
        "w1_scales": packed_w1[1],
        "ga": (np.random.uniform(0.5, 1.5, (H, 1)) * u[:, None]).astype(np.float32),
        "gb": (np.random.uniform(0.5, 1.5, (H, 1)) / u[:, None]).astype(np.float32),
        "offs": striped(np.random.permutation(T)[:S]),
        "n1": striped8(perm[:, :W]),
        "n2": striped8(perm[:, W:]),
        "n3": striped8(np.stack([np.random.permutation(S) for _ in range(8)])),
        "n4": striped8(np.stack([np.random.permutation(S) for _ in range(8)])),
        "n5": striped8(np.stack([np.random.permutation(S) for _ in range(8)])),
        "n6": striped8(np.stack([np.random.permutation(S) for _ in range(8)])),
    }


def reference(x_words, x_scales, w1_words, w1_scales, ga, gb, offs, n1, n2, n3, n4, n5, n6):
    xq = unpack_weight(x_words, x_scales)[:, unstriped(offs)]
    y = unpack_weight(w1_words, w1_scales).T @ xq
    pa = y[np.arange(H)[:, None], runs(n1, H)]
    pb = y[np.arange(H)[:, None], runs(n2, H)]
    rb = np.maximum(pa, pb)
    ra = pa / (np.abs(pb) + 0.5)
    ds = np.zeros((H, S))
    ds[np.arange(H)[:, None], runs(n1, H)] = ra
    dt = ds.copy()
    dt[np.arange(H)[:, None], runs(n2, H)] = rb
    z = f64(ga) * dt
    ex = np.exp(0.5 * y)
    z2 = f64(gb) * ((2.0 * ex) / (ex + ex[np.arange(H)[:, None], runs(n3, H)] + ex[np.arange(H)[:, None], runs(n4, H)]))
    s = 0.0625 * ((mxq(z, 0, "e4m3").T @ mxq(z2, 0, "e4m3")))
    out_0 = s * (s[np.arange(S)[:, None], runs(n5, S)] - (s[np.arange(S)[:, None], runs(n6, S)]))
    return (out_0,) + planes(out_0)

@@ -1,0 +1,221 @@
+from contextlib import ExitStack
+
+import concourse.mybir as mybir
+from concourse.masks import make_identity
+
+F32 = mybir.dt.float32
+BF16 = mybir.dt.bfloat16
+I32 = mybir.dt.int32
+U32 = mybir.dt.uint32
+U16 = mybir.dt.uint16
+U8 = mybir.dt.uint8
+FP8X4 = mybir.dt.float8_e4m3fn_x4
+ACT = mybir.ActivationFunctionType
+ALU = mybir.AluOpType
+
+P = 128
+PACK = 4
+K, T, S, H, W = 512, 2048, 512, 512, 256
+FLOPS = 2 * K * H * S + 2 * H * S * S
+VECTOR_N4_TILES = 2
+OUT_CHUNKS = (256, 128, 128)
+
+
+def tile_picked_selfratiosharewind_none_po_kernel(
+    tc, x_words, x_scales, w1_words, w1_scales, ga, gb, offs, n1, n2, n3, n4, n5, n6, out_0, out_1, out_2
+):
+    nc = tc.nc
+    tiles = range(PACK)
+    halves = range(S // W)
+
+    with ExitStack() as ctx:
+        lists = ctx.enter_context(tc.tile_pool(name="lists", bufs=1))
+        sb = ctx.enter_context(tc.tile_pool(name="sb", bufs=1))
+        psum = ctx.enter_context(tc.psum_pool(name="psum", bufs=1))
+
+        def list_tile(name, src):
+            return lists.tile(list(src.shape), U16, name=name)
+
+        offs_sb = list_tile("offs_sb", offs)
+        n1_sb = list_tile("n1_sb", n1)
+        n2_sb = list_tile("n2_sb", n2)
+        n3_sb = list_tile("n3_sb", n3)
+        n4_sb = list_tile("n4_sb", n4)
+        n5_sb = list_tile("n5_sb", n5)
+        n6_sb = list_tile("n6_sb", n6)
+
+        def entries(lst, first, count):
+            return lst[:, first // 16 : (first + count) // 16]
+
+        xw = sb.tile([P, T], I32, name="xw")
+        xs = sb.tile([P, T], U8, name="xs")
+        ww = sb.tile([P, H], I32, name="ww")
+        ws = sb.tile([P, H], U8, name="ws")
+        ga_sb = sb.tile([P, PACK], F32, name="ga_sb")
+        gb_sb = sb.tile([P, PACK], F32, name="gb_sb")
+
+        def load_scale_rows(queue, plane, rows, q):
+            queue.dma_start(plane[32 * q : 32 * q + 4, :].bitcast(I32), rows[0][4 * q : 4 * q + 4, :].bitcast(I32))
+
+        nc.vector.memset(ws[:].bitcast(I32), 0)
+        nc.vector.memset(xs[:].bitcast(I32), 0)
+        nc.sync.dma_start(offs_sb[:], offs)
+        nc.sync.dma_start(xw[:], x_words[0].rearrange("p n t -> p (n t)").bitcast(I32))
+        for q in range(4):
+            load_scale_rows(nc.sync, xs, x_scales, q)
+        nc.sync.dma_start(ww[:], w1_words[0].rearrange("p n t -> p (n t)").bitcast(I32))
+        for q in range(4):
+            load_scale_rows(nc.gpsimd if q < 2 else nc.sync, ws, w1_scales, q)
+        for dst, src in ((n1_sb, n1), (n2_sb, n2), (n3_sb, n3), (n4_sb, n4), (n5_sb, n5), (n6_sb, n6)):
+            nc.sync.dma_start(dst[:], src)
+        nc.sync.dma_start(ga_sb[:], ga.rearrange("(p t) o -> p (t o)", t=PACK))
+        nc.sync.dma_start(gb_sb[:], gb.rearrange("(p t) o -> p (t o)", t=PACK))
+        ident = sb.tile([P, P], F32, name="ident")
+        make_identity(nc, ident[:])
+
+        xg = sb.tile([P, S], U32, name="xg", align_bytes=64)
+        xgs = sb.tile([P, S], U8, name="xgs", align_bytes=64)
+        wd = sb.tile([P, H], I32, name="wd", align_bytes=64)
+        wds = sb.tile([P, H], U8, name="wds", align_bytes=64)
+        nc.vector.tensor_copy(xgs[:], xs[:].indirect(offs_sb[:]))
+        nc.vector.tensor_copy(wds[:].rearrange("p (t m) -> p m t", t=PACK), ws[:].rearrange("p (m t) -> p m t", t=PACK))
+        nc.vector.tensor_copy(wd[:].rearrange("p (t m) -> p m t", t=PACK), ww[:].rearrange("p (m t) -> p m t", t=PACK))
+        nc.vector.tensor_copy(xg[:], xw[:].bitcast(U32).indirect(offs_sb[:]))
+
+        y_ps = [psum.tile([P, S], F32, name=f"y_ps{t}", tag=f"a{t}") for t in tiles]
+        y = [sb.tile([P, S], F32, name=f"y{t}", tag=f"y{t}") for t in tiles]
+        ex = [sb.tile([P, S], F32, name=f"ex{t}") for t in tiles]
+        e3 = [sb.tile([P, S], F32, name=f"e3_{t}") for t in tiles]
+        e4 = [sb.tile([P, S], F32, name=f"e4_{t}") for t in tiles]
+        pa = sb.tile([P, PACK * W], F32, name="pa")
+        pb = sb.tile([P, PACK * W], F32, name="pb")
+        rb = sb.tile([P, PACK * W], F32, name="rb")
+        den = sb.tile([P, PACK * W], F32, name="den")
+        den2 = sb.tile([P, PACK * W], F32, name="den2")
+        dt = [sb.tile([P, S], F32, name=f"dt{t}") for t in tiles]
+
+        def pairs(t):
+            return slice(t * W, (t + 1) * W)
+
+        def block(b):
+            return slice(b * P, (b + 1) * P)
+
+        for t in tiles:
+            nc.tensor.matmul_mx(
+                out=y_ps[t][:], lhsT=wd[:, block(t)].bitcast(FP8X4), lhsT_scale=wds[:, block(t)],
+                rhs=xg[:].bitcast(FP8X4), rhs_scale=xgs[:], start=True, stop=True,
+            )
+            nc.scalar.copy(y[t][:], y_ps[t][:])
+        for t in tiles:
+            nc.vector.tensor_copy(pa[:, pairs(t)], y[t][:].indirect(n1_sb[:]))
+            nc.vector.tensor_copy(pb[:, pairs(t)], y[t][:].indirect(n2_sb[:]))
+
+        for t in tiles:
+            nc.scalar.activation(ex[t][:], y_ps[t][:], ACT.Exp, scale=0.5)
+            for h in halves:
+                cols = slice(h * W, (h + 1) * W)
+                nc.scalar.activation(e3[t][:, cols], y[t][:].indirect(entries(n3_sb, h * W, W)), ACT.Exp, scale=0.5)
+            for h in halves:
+                cols = slice(h * W, (h + 1) * W)
+                if t < VECTOR_N4_TILES:
+                    nc.vector.tensor_tensor(e4[t][:, cols], ex[t][:].indirect(entries(n4_sb, h * W, W)), e3[t][:, cols], ALU.add)
+                else:
+                    nc.scalar.activation(e4[t][:, cols], y[t][:].indirect(entries(n4_sb, h * W, W)), ACT.Exp, scale=0.5)
+            if t == 1:
+                nc.scalar.activation(den[:], pb[:], ACT.Abs)
+                nc.scalar.activation(den2[:], den[:], ACT.Square, bias=0.5)
+
+        nc.vector.tensor_tensor(rb[:], pa[:], pb[:], ALU.max)
+        for t in tiles:
+            nc.vector.tensor_copy(dt[t][:].indirect(n2_sb[:]), rb[:, pairs(t)])
+
+        sum_ps = [psum.tile([P, S], F32, name=f"sum_ps{b}", tag=f"b{b}") for b in tiles]
+        for t in tiles:
+            terms = [ex[t], e4[t]] if t < VECTOR_N4_TILES else [ex[t], e3[t], e4[t]]
+            for b in tiles:
+                for i, term in enumerate(terms):
+                    nc.tensor.matmul(
+                        sum_ps[b][:, block(t)], term[:, block(b)], ident[:],
+                        start=(i == 0), stop=(i == len(terms) - 1), is_transpose=True,
+                    )
+
+        inv = sb.tile([P, PACK * W], F32, name="inv", tag=f"y{PACK - 1}")
+        for t in tiles:
+            nc.scalar.activation(inv[:, pairs(t)], den2[:, pairs(t)], ACT.Abs_reciprocal_sqrt)
+        root = [sb.tile([P, S], F32, name=f"root{b}") for b in tiles]
+        for b in tiles:
+            nc.scalar.activation(root[b][:], sum_ps[b][:], ACT.Abs_reciprocal_sqrt, scale=0.5)
+        back_ps = [psum.tile([P, S], F32, name=f"back_ps{t}", tag=f"a{t}") for t in tiles]
+        share = [sb.tile([P, S], F32, name=f"share{t}") for t in tiles]
+        zp = sb.tile([P, PACK, S], BF16, name="zp")
+        z2p = sb.tile([P, PACK, S], BF16, name="z2p")
+        for t in tiles:
+            for b in tiles:
+                nc.tensor.transpose(back_ps[t][:, block(b)], root[b][:, block(t)], ident[:])
+            nc.scalar.activation(share[t][:], back_ps[t][:], ACT.Square)
+
+        def scatter_ra(t):
+            nc.vector.tensor_tensor(dt[t][:].indirect(n1_sb[:]), pa[:, pairs(t)], inv[:, pairs(t)], ALU.mult)
+            nc.scalar.activation(
+                zp[:, t, :].rearrange("p (u m) -> p m u", u=PACK), dt[t][:].rearrange("p (m u) -> p m u", u=PACK),
+                ACT.Copy, scale=ga_sb[:, t : t + 1],
+            )
+
+        for t in range(PACK - 1):
+            scatter_ra(t)
+        for t in tiles:
+            nc.vector.scalar_tensor_tensor(z2p[:, t, :], share[t][:], gb_sb[:, t : t + 1], ex[t][:], ALU.mult, ALU.mult)
+        scatter_ra(PACK - 1)
+
+        z2i = sb.tile([P, S, PACK], BF16, name="z2i", align_bytes=64)
+        z2c = sb.tile([P, S], U32, name="z2c", align_bytes=64)
+        z2s = sb.tile([P, S], U8, name="z2s", align_bytes=64)
+        nc.scalar.copy(
+            z2i[:].rearrange("p (c i) t -> p c t i", i=4), z2p[:].rearrange("p t (c i) -> p c t i", i=4)
+        )
+        nc.vector.quantize_mx(out=z2c[:].bitcast(FP8X4), scales=z2s[:], in_=z2i[:].rearrange("p j t -> p (j t)"))
+
+        zi = [sb.tile([P, P, PACK], BF16, name=f"zi{u}", align_bytes=64) for u in tiles]
+        zc = [sb.tile([P, P], U32, name=f"zc{u}", align_bytes=64) for u in tiles]
+        zs = [sb.tile([P, P], U8, name=f"zs{u}", align_bytes=64) for u in tiles]
+        s_ps = [psum.tile([P, S], F32, name=f"s_ps{u}", tag=f"b{u}") for u in tiles]
+        s = [sb.tile([P, S], F32, name=f"s{u}") for u in tiles]
+        for u in tiles:
+            nc.vector.tensor_copy(
+                zi[u][:].rearrange("p (c i) t -> p c t i", i=4), zp[:, :, block(u)].rearrange("p t (c i) -> p c t i", i=4)
+            )
+        for u in tiles:
+            nc.vector.quantize_mx(out=zc[u][:].bitcast(FP8X4), scales=zs[u][:], in_=zi[u][:].rearrange("p m t -> p (m t)"))
+            nc.tensor.matmul_mx(
+                out=s_ps[u][:], lhsT=zc[u][:].bitcast(FP8X4), lhsT_scale=zs[u][:],
+                rhs=z2c[:].bitcast(FP8X4), rhs_scale=z2s[:], start=True, stop=True,
+            )
+            nc.scalar.activation(s[u][:], s_ps[u][:], ACT.Copy, scale=0.0625)
+
+        out_rows = out_0.rearrange("(p u) j -> p u j", u=PACK)
+        out_words = out_1[0].rearrange("p n t -> p (n t)").bitcast(I32)
+        oc = sb.tile([P, S], I32, name="oc", align_bytes=64)
+        osc = sb.tile([P, S], U8, name="osc", align_bytes=64)
+        first = 0
+        for c, width in enumerate(OUT_CHUNKS):
+            cols = slice(first, first + width)
+            g6 = [sb.tile([P, width], F32, name=f"g6_{c}_{u}") for u in tiles]
+            d = [sb.tile([P, width], F32, name=f"d_{c}_{u}") for u in tiles]
+            o = sb.tile([P, PACK, width], F32, name=f"o{c}")
+            ob = sb.tile([P, width, PACK], BF16, name=f"ob{c}", align_bytes=64)
+            for u in tiles:
+                nc.vector.tensor_copy(g6[u][:], s[u][:].indirect(entries(n6_sb, first, width)))
+            for u in tiles:
+                nc.vector.tensor_tensor(d[u][:], s[u][:].indirect(entries(n5_sb, first, width)), g6[u][:], ALU.subtract)
+            for u in tiles:
+                nc.vector.tensor_tensor(o[:, u, :], d[u][:], s[u][:, cols], ALU.mult)
+            nc.sync.dma_start(out_rows[:, :, cols], o[:])
+            nc.scalar.copy(ob[:], o[:].rearrange("p u j -> p j u"))
+            nc.vector.quantize_mx(
+                out=oc[:, cols].bitcast(FP8X4), scales=osc[:, cols], in_=ob[:].rearrange("p j u -> p (j u)")
+            )
+            nc.sync.dma_start(out_words[:, cols], oc[:, cols])
+            first = first + width
+        for q in range(4):
+            eng = nc.sync if q % 2 == 0 else nc.scalar
+            eng.dma_start(out_2[0][4 * q : 4 * q + 4, :].bitcast(I32), osc[32 * q : 32 * q + 4, :].bitcast(I32))

@@ -18,7 +18,6 @@ PACK = 4
 K, T, S, H, W = 512, 2048, 512, 512, 256
 FLOPS = 2 * K * H * S + 2 * H * S * S
 VECTOR_N4_TILES = 2
-OUT_CHUNKS = (256, 128, 128)
 
 
 def tile_picked_selfratiosharewind_none_po_kernel(
@@ -47,9 +46,12 @@ def tile_picked_selfratiosharewind_none_po_kernel(
         def entries(lst, first, count):
             return lst[:, first // 16 : (first + count) // 16]
 
+        def half(h):
+            return slice(h * W, (h + 1) * W)
+
         xw = sb.tile([P, T], I32, name="xw")
         xs = sb.tile([P, T], U8, name="xs")
-        ww = sb.tile([P, H], I32, name="ww")
+        ww = sb.tile([P, H], I32, name="ww", tag="ww")
         ws = sb.tile([P, H], U8, name="ws")
         ga_sb = sb.tile([P, PACK], F32, name="ga_sb")
         gb_sb = sb.tile([P, PACK], F32, name="gb_sb")
@@ -57,30 +59,32 @@ def tile_picked_selfratiosharewind_none_po_kernel(
         def load_scale_rows(queue, plane, rows, q):
             queue.dma_start(plane[32 * q : 32 * q + 4, :].bitcast(I32), rows[0][4 * q : 4 * q + 4, :].bitcast(I32))
 
-        nc.vector.memset(ws[:].bitcast(I32), 0)
+        nc.gpsimd.memset(ws[:].bitcast(I32), 0)
         nc.vector.memset(xs[:].bitcast(I32), 0)
         nc.sync.dma_start(offs_sb[:], offs)
-        nc.sync.dma_start(xw[:], x_words[0].rearrange("p n t -> p (n t)").bitcast(I32))
-        for q in range(4):
-            load_scale_rows(nc.sync, xs, x_scales, q)
+        nc.scalar.dma_start(xw[:], x_words[0].rearrange("p n t -> p (n t)").bitcast(I32))
         nc.sync.dma_start(ww[:], w1_words[0].rearrange("p n t -> p (n t)").bitcast(I32))
         for q in range(4):
-            load_scale_rows(nc.gpsimd if q < 2 else nc.sync, ws, w1_scales, q)
+            load_scale_rows(nc.sync, xs, x_scales, q)
+        for q in range(4):
+            load_scale_rows(nc.gpsimd if q < 3 else nc.sync, ws, w1_scales, q)
         for dst, src in ((n1_sb, n1), (n2_sb, n2), (n3_sb, n3), (n4_sb, n4), (n5_sb, n5), (n6_sb, n6)):
             nc.sync.dma_start(dst[:], src)
         nc.sync.dma_start(ga_sb[:], ga.rearrange("(p t) o -> p (t o)", t=PACK))
         nc.sync.dma_start(gb_sb[:], gb.rearrange("(p t) o -> p (t o)", t=PACK))
-        ident = sb.tile([P, P], F32, name="ident")
-        make_identity(nc, ident[:])
 
         xg = sb.tile([P, S], U32, name="xg", align_bytes=64)
         xgs = sb.tile([P, S], U8, name="xgs", align_bytes=64)
         wd = sb.tile([P, H], I32, name="wd", align_bytes=64)
         wds = sb.tile([P, H], U8, name="wds", align_bytes=64)
+        nc.vector.tensor_copy(wd[:].rearrange("p (t m) -> p m t", t=PACK), ww[:].rearrange("p (m t) -> p m t", t=PACK))
         nc.vector.tensor_copy(xgs[:], xs[:].indirect(offs_sb[:]))
         nc.vector.tensor_copy(wds[:].rearrange("p (t m) -> p m t", t=PACK), ws[:].rearrange("p (m t) -> p m t", t=PACK))
-        nc.vector.tensor_copy(wd[:].rearrange("p (t m) -> p m t", t=PACK), ww[:].rearrange("p (m t) -> p m t", t=PACK))
-        nc.vector.tensor_copy(xg[:], xw[:].bitcast(U32).indirect(offs_sb[:]))
+        for h in halves:
+            nc.vector.tensor_copy(xg[:, half(h)], xw[:].bitcast(U32).indirect(entries(offs_sb, h * W, W)))
+
+        ident = sb.tile([P, P], F32, name="ident", tag="ww")
+        make_identity(nc, ident[:])
 
         y_ps = [psum.tile([P, S], F32, name=f"y_ps{t}", tag=f"a{t}") for t in tiles]
         y = [sb.tile([P, S], F32, name=f"y{t}", tag=f"y{t}") for t in tiles]
@@ -91,7 +95,6 @@ def tile_picked_selfratiosharewind_none_po_kernel(
         pb = sb.tile([P, PACK * W], F32, name="pb")
         rb = sb.tile([P, PACK * W], F32, name="rb")
         den = sb.tile([P, PACK * W], F32, name="den")
-        den2 = sb.tile([P, PACK * W], F32, name="den2")
         dt = [sb.tile([P, S], F32, name=f"dt{t}") for t in tiles]
 
         def pairs(t):
@@ -101,10 +104,11 @@ def tile_picked_selfratiosharewind_none_po_kernel(
             return slice(b * P, (b + 1) * P)
 
         for t in tiles:
-            nc.tensor.matmul_mx(
-                out=y_ps[t][:], lhsT=wd[:, block(t)].bitcast(FP8X4), lhsT_scale=wds[:, block(t)],
-                rhs=xg[:].bitcast(FP8X4), rhs_scale=xgs[:], start=True, stop=True,
-            )
+            for h in halves:
+                nc.tensor.matmul_mx(
+                    out=y_ps[t][:, half(h)], lhsT=wd[:, block(t)].bitcast(FP8X4), lhsT_scale=wds[:, block(t)],
+                    rhs=xg[:, half(h)].bitcast(FP8X4), rhs_scale=xgs[:, half(h)], start=True, stop=True,
+                )
             nc.scalar.copy(y[t][:], y_ps[t][:])
         for t in tiles:
             nc.vector.tensor_copy(pa[:, pairs(t)], y[t][:].indirect(n1_sb[:]))
@@ -123,7 +127,6 @@ def tile_picked_selfratiosharewind_none_po_kernel(
                     nc.scalar.activation(e4[t][:, cols], y[t][:].indirect(entries(n4_sb, h * W, W)), ACT.Exp, scale=0.5)
             if t == 1:
                 nc.scalar.activation(den[:], pb[:], ACT.Abs)
-                nc.scalar.activation(den2[:], den[:], ACT.Square, bias=0.5)
 
         nc.vector.tensor_tensor(rb[:], pa[:], pb[:], ALU.max)
         for t in tiles:
@@ -139,9 +142,11 @@ def tile_picked_selfratiosharewind_none_po_kernel(
                         start=(i == 0), stop=(i == len(terms) - 1), is_transpose=True,
                     )
 
-        inv = sb.tile([P, PACK * W], F32, name="inv", tag=f"y{PACK - 1}")
+        den2 = sb.tile([P, PACK * W], F32, name="den2", tag=f"y{PACK - 1}")
+        inv = sb.tile([P, PACK * W], F32, name="inv")
         for t in tiles:
-            nc.scalar.activation(inv[:, pairs(t)], den2[:, pairs(t)], ACT.Abs_reciprocal_sqrt)
+            nc.scalar.activation(den2[:, pairs(t)], den[:, pairs(t)], ACT.Abs_reciprocal_sqrt, bias=0.5)
+            nc.scalar.activation(inv[:, pairs(t)], den2[:, pairs(t)], ACT.Square)
         root = [sb.tile([P, S], F32, name=f"root{b}") for b in tiles]
         for b in tiles:
             nc.scalar.activation(root[b][:], sum_ps[b][:], ACT.Abs_reciprocal_sqrt, scale=0.5)
@@ -161,61 +166,78 @@ def tile_picked_selfratiosharewind_none_po_kernel(
                 ACT.Copy, scale=ga_sb[:, t : t + 1],
             )
 
-        for t in range(PACK - 1):
+        for t in tiles:
             scatter_ra(t)
         for t in tiles:
             nc.vector.scalar_tensor_tensor(z2p[:, t, :], share[t][:], gb_sb[:, t : t + 1], ex[t][:], ALU.mult, ALU.mult)
-        scatter_ra(PACK - 1)
-
-        z2i = sb.tile([P, S, PACK], BF16, name="z2i", align_bytes=64)
-        z2c = sb.tile([P, S], U32, name="z2c", align_bytes=64)
-        z2s = sb.tile([P, S], U8, name="z2s", align_bytes=64)
-        nc.scalar.copy(
-            z2i[:].rearrange("p (c i) t -> p c t i", i=4), z2p[:].rearrange("p t (c i) -> p c t i", i=4)
-        )
-        nc.vector.quantize_mx(out=z2c[:].bitcast(FP8X4), scales=z2s[:], in_=z2i[:].rearrange("p j t -> p (j t)"))
 
         zi = [sb.tile([P, P, PACK], BF16, name=f"zi{u}", align_bytes=64) for u in tiles]
         zc = [sb.tile([P, P], U32, name=f"zc{u}", align_bytes=64) for u in tiles]
         zs = [sb.tile([P, P], U8, name=f"zs{u}", align_bytes=64) for u in tiles]
-        s_ps = [psum.tile([P, S], F32, name=f"s_ps{u}", tag=f"b{u}") for u in tiles]
-        s = [sb.tile([P, S], F32, name=f"s{u}") for u in tiles]
         for u in tiles:
-            nc.vector.tensor_copy(
+            nc.scalar.copy(
                 zi[u][:].rearrange("p (c i) t -> p c t i", i=4), zp[:, :, block(u)].rearrange("p t (c i) -> p c t i", i=4)
             )
-        for u in tiles:
             nc.vector.quantize_mx(out=zc[u][:].bitcast(FP8X4), scales=zs[u][:], in_=zi[u][:].rearrange("p m t -> p (m t)"))
-            nc.tensor.matmul_mx(
-                out=s_ps[u][:], lhsT=zc[u][:].bitcast(FP8X4), lhsT_scale=zs[u][:],
-                rhs=z2c[:].bitcast(FP8X4), rhs_scale=z2s[:], start=True, stop=True,
+
+        z2i = [sb.tile([P, W, PACK], BF16, name=f"z2i{h}", align_bytes=64) for h in halves]
+        z2c = [sb.tile([P, W], U32, name=f"z2c{h}", align_bytes=64) for h in halves]
+        z2s = [sb.tile([P, W], U8, name=f"z2s{h}", align_bytes=64) for h in halves]
+        for h in halves:
+            nc.vector.tensor_copy(
+                z2i[h][:].rearrange("p (c i) t -> p c t i", i=4), z2p[:, :, half(h)].rearrange("p t (c i) -> p c t i", i=4)
             )
-            nc.scalar.activation(s[u][:], s_ps[u][:], ACT.Copy, scale=0.0625)
+        for h in halves:
+            nc.vector.quantize_mx(out=z2c[h][:].bitcast(FP8X4), scales=z2s[h][:], in_=z2i[h][:].rearrange("p j t -> p (j t)"))
+
+        s_ps = [[psum.tile([P, W], F32, name=f"s_ps{u}_{h}", tag=f"{'ab'[h]}{u}") for h in halves] for u in tiles]
+        s = [sb.tile([P, S], F32, name=f"s{u}") for u in tiles]
+        for u in tiles:
+            for h in halves:
+                nc.tensor.matmul_mx(
+                    out=s_ps[u][h][:], lhsT=zc[u][:].bitcast(FP8X4), lhsT_scale=zs[u][:],
+                    rhs=z2c[h][:].bitcast(FP8X4), rhs_scale=z2s[h][:], start=True, stop=True,
+                )
+                nc.scalar.activation(s[u][:, half(h)], s_ps[u][h][:], ACT.Copy, scale=0.0625)
 
         out_rows = out_0.rearrange("(p u) j -> p u j", u=PACK)
         out_words = out_1[0].rearrange("p n t -> p (n t)").bitcast(I32)
         oc = sb.tile([P, S], I32, name="oc", align_bytes=64)
         osc = sb.tile([P, S], U8, name="osc", align_bytes=64)
-        first = 0
-        for c, width in enumerate(OUT_CHUNKS):
-            cols = slice(first, first + width)
-            g6 = [sb.tile([P, width], F32, name=f"g6_{c}_{u}") for u in tiles]
-            d = [sb.tile([P, width], F32, name=f"d_{c}_{u}") for u in tiles]
-            o = sb.tile([P, PACK, width], F32, name=f"o{c}")
-            ob = sb.tile([P, width, PACK], BF16, name=f"ob{c}", align_bytes=64)
-            for u in tiles:
-                nc.vector.tensor_copy(g6[u][:], s[u][:].indirect(entries(n6_sb, first, width)))
-            for u in tiles:
-                nc.vector.tensor_tensor(d[u][:], s[u][:].indirect(entries(n5_sb, first, width)), g6[u][:], ALU.subtract)
-            for u in tiles:
-                nc.vector.tensor_tensor(o[:, u, :], d[u][:], s[u][:, cols], ALU.mult)
-            nc.sync.dma_start(out_rows[:, :, cols], o[:])
-            nc.scalar.copy(ob[:], o[:].rearrange("p u j -> p j u"))
-            nc.vector.quantize_mx(
-                out=oc[:, cols].bitcast(FP8X4), scales=osc[:, cols], in_=ob[:].rearrange("p j u -> p (j u)")
+        chunks = range(S // P)
+        last = PACK - 1
+        o = sb.tile([P, S // P, PACK, P], F32, name="o")
+        for u in range(last):
+            g6 = sb.tile([P, S], F32, name=f"g6_{u}")
+            d = sb.tile([P, S], F32, name=f"d_{u}")
+            for h in halves:
+                nc.vector.tensor_copy(g6[:, half(h)], s[u][:].indirect(entries(n6_sb, h * W, W)))
+            for h in halves:
+                nc.vector.tensor_tensor(d[:, half(h)], s[u][:].indirect(entries(n5_sb, h * W, W)), g6[:, half(h)], ALU.subtract)
+            nc.gpsimd.tensor_tensor(
+                o[:, :, u, :], d[:].rearrange("p (c j) -> p c j", j=P), s[u][:].rearrange("p (c j) -> p c j", j=P), ALU.mult
             )
-            nc.sync.dma_start(out_words[:, cols], oc[:, cols])
-            first = first + width
+            nc.sync.dma_start(out_rows[:, u, :].rearrange("p (c j) -> p c j", j=P), o[:, :, u, :])
+        g6 = sb.tile([P, S], F32, name="g6_last")
+        d = sb.tile([P, S], F32, name="d_last")
+        for h in halves:
+            nc.vector.tensor_copy(g6[:, half(h)], s[last][:].indirect(entries(n6_sb, h * W, W)))
+        for c in chunks:
+            nc.vector.tensor_tensor(d[:, block(c)], s[last][:].indirect(entries(n5_sb, c * P, P)), g6[:, block(c)], ALU.subtract)
+            nc.vector.tensor_tensor(o[:, c, last, :], d[:, block(c)], s[last][:, block(c)], ALU.mult)
+        for c in chunks:
+            ob = sb.tile([P, P, PACK], BF16, name=f"ob{c}", align_bytes=64)
+            nc.scalar.copy(ob[:], o[:, c].rearrange("p u j -> p j u"))
+            nc.vector.quantize_mx(
+                out=oc[:, block(c)].bitcast(FP8X4), scales=osc[:, block(c)], in_=ob[:].rearrange("p j u -> p (j u)")
+            )
+        for h in halves:
+            nc.sync.dma_start(
+                out_rows[:, last, half(h)].rearrange("p (c j) -> p c j", j=P), o[:, 2 * h : 2 * h + 2, last, :]
+            )
+        early = slice(0, S - P)
+        nc.sync.dma_start(out_words[:, early], oc[:, early])
+        nc.sync.dma_start(out_words[:, block(chunks[-1])], oc[:, block(chunks[-1])])
         for q in range(4):
             eng = nc.sync if q % 2 == 0 else nc.scalar
             eng.dma_start(out_2[0][4 * q : 4 * q + 4, :].bitcast(I32), osc[32 * q : 32 * q + 4, :].bitcast(I32))

@@ -86,7 +86,12 @@ def tile_picked_selfratiosharewind_none_po_kernel(
         ident = sb.tile([P, P], F32, name="ident", tag="ww")
         make_identity(nc, ident[:])
 
-        y_ps = [psum.tile([P, S], F32, name=f"y_ps{t}", tag=f"a{t}") for t in tiles]
+        def result_banks(name):
+            banks = [[(psum.tile([P, S], F32, name=f"{name}{t}", tag=f"a{t}"), slice(0, S))] for t in range(1, PACK)]
+            first = [(psum.tile([P, W], F32, name=f"{name}0_{h}", tag=f"{'ab'[h]}0"), half(h)) for h in halves]
+            return [first] + banks
+
+        y_ps = result_banks("y_ps")
         y = [sb.tile([P, S], F32, name=f"y{t}", tag=f"y{t}") for t in tiles]
         ex = [sb.tile([P, S], F32, name=f"ex{t}") for t in tiles]
         e3 = [sb.tile([P, S], F32, name=f"e3_{t}") for t in tiles]
@@ -94,7 +99,6 @@ def tile_picked_selfratiosharewind_none_po_kernel(
         pa = sb.tile([P, PACK * W], F32, name="pa")
         pb = sb.tile([P, PACK * W], F32, name="pb")
         rb = sb.tile([P, PACK * W], F32, name="rb")
-        den = sb.tile([P, PACK * W], F32, name="den")
         dt = [sb.tile([P, S], F32, name=f"dt{t}") for t in tiles]
 
         def pairs(t):
@@ -104,59 +108,63 @@ def tile_picked_selfratiosharewind_none_po_kernel(
             return slice(b * P, (b + 1) * P)
 
         for t in tiles:
-            for h in halves:
+            for bank, cols in y_ps[t]:
                 nc.tensor.matmul_mx(
-                    out=y_ps[t][:, half(h)], lhsT=wd[:, block(t)].bitcast(FP8X4), lhsT_scale=wds[:, block(t)],
-                    rhs=xg[:, half(h)].bitcast(FP8X4), rhs_scale=xgs[:, half(h)], start=True, stop=True,
+                    out=bank[:], lhsT=wd[:, block(t)].bitcast(FP8X4), lhsT_scale=wds[:, block(t)],
+                    rhs=xg[:, cols].bitcast(FP8X4), rhs_scale=xgs[:, cols], start=True, stop=True,
                 )
-            nc.scalar.copy(y[t][:], y_ps[t][:])
+                nc.scalar.copy(y[t][:, cols], bank[:])
         for t in tiles:
             nc.vector.tensor_copy(pa[:, pairs(t)], y[t][:].indirect(n1_sb[:]))
             nc.vector.tensor_copy(pb[:, pairs(t)], y[t][:].indirect(n2_sb[:]))
 
         for t in tiles:
-            nc.scalar.activation(ex[t][:], y_ps[t][:], ACT.Exp, scale=0.5)
+            for bank, cols in y_ps[t]:
+                nc.scalar.activation(ex[t][:, cols], bank[:], ACT.Exp, scale=0.5)
             for h in halves:
                 cols = slice(h * W, (h + 1) * W)
                 nc.scalar.activation(e3[t][:, cols], y[t][:].indirect(entries(n3_sb, h * W, W)), ACT.Exp, scale=0.5)
             for h in halves:
                 cols = slice(h * W, (h + 1) * W)
-                if t < VECTOR_N4_TILES:
-                    nc.vector.tensor_tensor(e4[t][:, cols], ex[t][:].indirect(entries(n4_sb, h * W, W)), e3[t][:, cols], ALU.add)
-                else:
+                if t < PACK - VECTOR_N4_TILES:
                     nc.scalar.activation(e4[t][:, cols], y[t][:].indirect(entries(n4_sb, h * W, W)), ACT.Exp, scale=0.5)
-            if t == 1:
-                nc.scalar.activation(den[:], pb[:], ACT.Abs)
 
         nc.vector.tensor_tensor(rb[:], pa[:], pb[:], ALU.max)
         for t in tiles:
             nc.vector.tensor_copy(dt[t][:].indirect(n2_sb[:]), rb[:, pairs(t)])
+        for t in range(PACK - VECTOR_N4_TILES, PACK):
+            for h in halves:
+                nc.vector.tensor_tensor(
+                    e4[t][:, half(h)], ex[t][:].indirect(entries(n4_sb, h * W, W)), e3[t][:, half(h)], ALU.add
+                )
 
         sum_ps = [psum.tile([P, S], F32, name=f"sum_ps{b}", tag=f"b{b}") for b in tiles]
         for t in tiles:
-            terms = [ex[t], e4[t]] if t < VECTOR_N4_TILES else [ex[t], e3[t], e4[t]]
+            terms = [ex[t], e4[t]] if t >= PACK - VECTOR_N4_TILES else [ex[t], e3[t], e4[t]]
             for b in tiles:
                 for i, term in enumerate(terms):
                     nc.tensor.matmul(
-                        sum_ps[b][:, block(t)], term[:, block(b)], ident[:],
+                        sum_ps[t][:, block(b)], term[:, block(b)], ident[:],
                         start=(i == 0), stop=(i == len(terms) - 1), is_transpose=True,
                     )
 
-        den2 = sb.tile([P, PACK * W], F32, name="den2", tag=f"y{PACK - 1}")
+        roots = sb.tile([P, PACK * (W + S)], F32, name="roots", tag=f"y{PACK - 1}")
+        den = sb.tile([P, PACK * W], F32, name="den")
         inv = sb.tile([P, PACK * W], F32, name="inv")
         for t in tiles:
-            nc.scalar.activation(den2[:, pairs(t)], den[:, pairs(t)], ACT.Abs_reciprocal_sqrt, bias=0.5)
-            nc.scalar.activation(inv[:, pairs(t)], den2[:, pairs(t)], ACT.Square)
-        root = [sb.tile([P, S], F32, name=f"root{b}") for b in tiles]
-        for b in tiles:
-            nc.scalar.activation(root[b][:], sum_ps[b][:], ACT.Abs_reciprocal_sqrt, scale=0.5)
+            nc.scalar.activation(roots[:, pairs(t)], pb[:, pairs(t)], ACT.Abs)
+            nc.scalar.activation(den[:, pairs(t)], roots[:, pairs(t)], ACT.Abs_reciprocal_sqrt, bias=0.5)
+            nc.scalar.activation(inv[:, pairs(t)], den[:, pairs(t)], ACT.Square)
+        root = [roots[:, PACK * W + t * S : PACK * W + (t + 1) * S] for t in tiles]
         back_ps = [psum.tile([P, S], F32, name=f"back_ps{t}", tag=f"a{t}") for t in tiles]
         share = [sb.tile([P, S], F32, name=f"share{t}") for t in tiles]
         zp = sb.tile([P, PACK, S], BF16, name="zp")
         z2p = sb.tile([P, PACK, S], BF16, name="z2p")
         for t in tiles:
+            nc.scalar.activation(root[t], sum_ps[t][:], ACT.Abs_reciprocal_sqrt, scale=0.5)
             for b in tiles:
-                nc.tensor.transpose(back_ps[t][:, block(b)], root[b][:, block(t)], ident[:])
+                nc.tensor.transpose(back_ps[t][:, block(b)], root[t][:, block(b)], ident[:])
+        for t in tiles:
             nc.scalar.activation(share[t][:], back_ps[t][:], ACT.Square)
 
         def scatter_ra(t):
@@ -171,34 +179,34 @@ def tile_picked_selfratiosharewind_none_po_kernel(
         for t in tiles:
             nc.vector.scalar_tensor_tensor(z2p[:, t, :], share[t][:], gb_sb[:, t : t + 1], ex[t][:], ALU.mult, ALU.mult)
 
-        zi = [sb.tile([P, P, PACK], BF16, name=f"zi{u}", align_bytes=64) for u in tiles]
-        zc = [sb.tile([P, P], U32, name=f"zc{u}", align_bytes=64) for u in tiles]
-        zs = [sb.tile([P, P], U8, name=f"zs{u}", align_bytes=64) for u in tiles]
-        for u in tiles:
-            nc.scalar.copy(
-                zi[u][:].rearrange("p (c i) t -> p c t i", i=4), zp[:, :, block(u)].rearrange("p t (c i) -> p c t i", i=4)
-            )
-            nc.vector.quantize_mx(out=zc[u][:].bitcast(FP8X4), scales=zs[u][:], in_=zi[u][:].rearrange("p m t -> p (m t)"))
-
         z2i = [sb.tile([P, W, PACK], BF16, name=f"z2i{h}", align_bytes=64) for h in halves]
-        z2c = [sb.tile([P, W], U32, name=f"z2c{h}", align_bytes=64) for h in halves]
-        z2s = [sb.tile([P, W], U8, name=f"z2s{h}", align_bytes=64) for h in halves]
+        z2c = sb.tile([P, S], U32, name="z2c", align_bytes=64)
+        z2s = sb.tile([P, S], U8, name="z2s", align_bytes=64)
         for h in halves:
             nc.vector.tensor_copy(
                 z2i[h][:].rearrange("p (c i) t -> p c t i", i=4), z2p[:, :, half(h)].rearrange("p t (c i) -> p c t i", i=4)
             )
         for h in halves:
-            nc.vector.quantize_mx(out=z2c[h][:].bitcast(FP8X4), scales=z2s[h][:], in_=z2i[h][:].rearrange("p j t -> p (j t)"))
+            nc.vector.quantize_mx(
+                out=z2c[:, half(h)].bitcast(FP8X4), scales=z2s[:, half(h)], in_=z2i[h][:].rearrange("p j t -> p (j t)")
+            )
 
-        s_ps = [[psum.tile([P, W], F32, name=f"s_ps{u}_{h}", tag=f"{'ab'[h]}{u}") for h in halves] for u in tiles]
+        zi = [sb.tile([P, P, PACK], BF16, name=f"zi{u}", align_bytes=64) for u in tiles]
+        zc = [sb.tile([P, P], U32, name=f"zc{u}", align_bytes=64) for u in tiles]
+        zs = [sb.tile([P, P], U8, name=f"zs{u}", align_bytes=64) for u in tiles]
+        s_ps = result_banks("s_ps")
         s = [sb.tile([P, S], F32, name=f"s{u}") for u in tiles]
         for u in tiles:
-            for h in halves:
+            nc.scalar.copy(
+                zi[u][:].rearrange("p (c i) t -> p c t i", i=4), zp[:, :, block(u)].rearrange("p t (c i) -> p c t i", i=4)
+            )
+            nc.vector.quantize_mx(out=zc[u][:].bitcast(FP8X4), scales=zs[u][:], in_=zi[u][:].rearrange("p m t -> p (m t)"))
+            for bank, cols in s_ps[u]:
                 nc.tensor.matmul_mx(
-                    out=s_ps[u][h][:], lhsT=zc[u][:].bitcast(FP8X4), lhsT_scale=zs[u][:],
-                    rhs=z2c[h][:].bitcast(FP8X4), rhs_scale=z2s[h][:], start=True, stop=True,
+                    out=bank[:], lhsT=zc[u][:].bitcast(FP8X4), lhsT_scale=zs[u][:],
+                    rhs=z2c[:, cols].bitcast(FP8X4), rhs_scale=z2s[:, cols], start=True, stop=True,
                 )
-                nc.scalar.activation(s[u][:, half(h)], s_ps[u][h][:], ACT.Copy, scale=0.0625)
+                nc.scalar.activation(s[u][:, cols], bank[:], ACT.Copy, scale=0.0625)
 
         out_rows = out_0.rearrange("(p u) j -> p u j", u=PACK)
         out_words = out_1[0].rearrange("p n t -> p (n t)").bitcast(I32)
@@ -214,17 +222,21 @@ def tile_picked_selfratiosharewind_none_po_kernel(
                 nc.vector.tensor_copy(g6[:, half(h)], s[u][:].indirect(entries(n6_sb, h * W, W)))
             for h in halves:
                 nc.vector.tensor_tensor(d[:, half(h)], s[u][:].indirect(entries(n5_sb, h * W, W)), g6[:, half(h)], ALU.subtract)
-            nc.gpsimd.tensor_tensor(
-                o[:, :, u, :], d[:].rearrange("p (c j) -> p c j", j=P), s[u][:].rearrange("p (c j) -> p c j", j=P), ALU.mult
-            )
+            for h in halves:
+                nc.vector.tensor_tensor(
+                    o[:, 2 * h : 2 * h + 2, u, :], d[:, half(h)].rearrange("p (c j) -> p c j", j=P),
+                    s[u][:, half(h)].rearrange("p (c j) -> p c j", j=P), ALU.mult,
+                )
             nc.sync.dma_start(out_rows[:, u, :].rearrange("p (c j) -> p c j", j=P), o[:, :, u, :])
         g6 = sb.tile([P, S], F32, name="g6_last")
         d = sb.tile([P, S], F32, name="d_last")
         for h in halves:
             nc.vector.tensor_copy(g6[:, half(h)], s[last][:].indirect(entries(n6_sb, h * W, W)))
-        for c in chunks:
-            nc.vector.tensor_tensor(d[:, block(c)], s[last][:].indirect(entries(n5_sb, c * P, P)), g6[:, block(c)], ALU.subtract)
-            nc.vector.tensor_tensor(o[:, c, last, :], d[:, block(c)], s[last][:, block(c)], ALU.mult)
+        for c in range(len(chunks) + 1):
+            if c < len(chunks):
+                nc.vector.tensor_tensor(d[:, block(c)], s[last][:].indirect(entries(n5_sb, c * P, P)), g6[:, block(c)], ALU.subtract)
+            if c > 0:
+                nc.vector.tensor_tensor(o[:, c - 1, last, :], d[:, block(c - 1)], s[last][:, block(c - 1)], ALU.mult)
         for c in chunks:
             ob = sb.tile([P, P, PACK], BF16, name=f"ob{c}", align_bytes=64)
             nc.scalar.copy(ob[:], o[:, c].rearrange("p u j -> p j u"))

@@ -15,9 +15,17 @@ ALU = mybir.AluOpType
 
 P = 128
 PACK = 4
-K, T, S, H, W = 512, 2048, 512, 512, 256
+QUADRANTS = 4
+LIST_ROWS = 16
+K, T, S, H = 512, 2048, 512, 512
+PAIRS = 256
+HALF = S // 2
+RUN = 4
 FLOPS = 2 * K * H * S + 2 * H * S * S
+
 VECTOR_N4_TILES = 2
+WHOLE_TILES = 2
+GPSIMD_SCALE_LOADS = 2
 
 
 def tile_picked_selfratiosharewind_none_po_kernel(
@@ -25,29 +33,44 @@ def tile_picked_selfratiosharewind_none_po_kernel(
 ):
     nc = tc.nc
     tiles = range(PACK)
-    halves = range(S // W)
+    halves = range(S // HALF)
+    blocks = range(S // P)
+    scalar_n4_tiles = range(PACK - VECTOR_N4_TILES)
+    vector_n4_tiles = range(PACK - VECTOR_N4_TILES, PACK)
+
+    def half(h):
+        return slice(h * HALF, (h + 1) * HALF)
+
+    def block(b):
+        return slice(b * P, (b + 1) * P)
+
+    def pairs(t):
+        return slice(t * PAIRS, (t + 1) * PAIRS)
+
+    def entries(list_tile, cols):
+        return list_tile[:, cols.start // LIST_ROWS : cols.stop // LIST_ROWS]
+
+    def words_of(packed):
+        return packed[0].rearrange("p n t -> p (n t)").bitcast(I32)
+
+    def scale_rows_in_hbm(rows, q):
+        return rows[0][4 * q : 4 * q + 4, :].bitcast(I32)
+
+    def scale_rows_in_sbuf(scale_tile, q):
+        return scale_tile[32 * q : 32 * q + 4, :].bitcast(I32)
 
     with ExitStack() as ctx:
         lists = ctx.enter_context(tc.tile_pool(name="lists", bufs=1))
         sb = ctx.enter_context(tc.tile_pool(name="sb", bufs=1))
         psum = ctx.enter_context(tc.psum_pool(name="psum", bufs=1))
 
-        def list_tile(name, src):
-            return lists.tile(list(src.shape), U16, name=name)
-
-        offs_sb = list_tile("offs_sb", offs)
-        n1_sb = list_tile("n1_sb", n1)
-        n2_sb = list_tile("n2_sb", n2)
-        n3_sb = list_tile("n3_sb", n3)
-        n4_sb = list_tile("n4_sb", n4)
-        n5_sb = list_tile("n5_sb", n5)
-        n6_sb = list_tile("n6_sb", n6)
-
-        def entries(lst, first, count):
-            return lst[:, first // 16 : (first + count) // 16]
-
-        def half(h):
-            return slice(h * W, (h + 1) * W)
+        offs_sb = lists.tile(list(offs.shape), U16, name="offs_sb")
+        n1_sb = lists.tile(list(n1.shape), U16, name="n1_sb")
+        n2_sb = lists.tile(list(n2.shape), U16, name="n2_sb")
+        n3_sb = lists.tile(list(n3.shape), U16, name="n3_sb")
+        n4_sb = lists.tile(list(n4.shape), U16, name="n4_sb")
+        n5_sb = lists.tile(list(n5.shape), U16, name="n5_sb")
+        n6_sb = lists.tile(list(n6.shape), U16, name="n6_sb")
 
         xw = sb.tile([P, T], I32, name="xw")
         xs = sb.tile([P, T], U8, name="xs")
@@ -56,20 +79,19 @@ def tile_picked_selfratiosharewind_none_po_kernel(
         ga_sb = sb.tile([P, PACK], F32, name="ga_sb")
         gb_sb = sb.tile([P, PACK], F32, name="gb_sb")
 
-        def load_scale_rows(queue, plane, rows, q):
-            queue.dma_start(plane[32 * q : 32 * q + 4, :].bitcast(I32), rows[0][4 * q : 4 * q + 4, :].bitcast(I32))
-
         nc.gpsimd.memset(ws[:].bitcast(I32), 0)
         nc.vector.memset(xs[:].bitcast(I32), 0)
         nc.sync.dma_start(offs_sb[:], offs)
-        nc.scalar.dma_start(xw[:], x_words[0].rearrange("p n t -> p (n t)").bitcast(I32))
-        nc.sync.dma_start(ww[:], w1_words[0].rearrange("p n t -> p (n t)").bitcast(I32))
-        for q in range(4):
-            load_scale_rows(nc.sync, xs, x_scales, q)
-        for q in range(4):
-            load_scale_rows(nc.gpsimd if q < 3 else nc.sync, ws, w1_scales, q)
-        for dst, src in ((n1_sb, n1), (n2_sb, n2), (n3_sb, n3), (n4_sb, n4), (n5_sb, n5), (n6_sb, n6)):
-            nc.sync.dma_start(dst[:], src)
+        nc.sync.dma_start(ww[:], words_of(w1_words))
+        for q in range(QUADRANTS):
+            nc.sync.dma_start(scale_rows_in_sbuf(xs, q), scale_rows_in_hbm(x_scales, q))
+        for q in range(QUADRANTS - 1):
+            queue = nc.gpsimd if q < GPSIMD_SCALE_LOADS else nc.sync
+            queue.dma_start(scale_rows_in_sbuf(ws, q), scale_rows_in_hbm(w1_scales, q))
+        nc.sync.dma_start(xw[:], words_of(x_words))
+        nc.sync.dma_start(scale_rows_in_sbuf(ws, QUADRANTS - 1), scale_rows_in_hbm(w1_scales, QUADRANTS - 1))
+        for list_tile, source in ((n1_sb, n1), (n2_sb, n2), (n3_sb, n3), (n4_sb, n4), (n5_sb, n5), (n6_sb, n6)):
+            nc.sync.dma_start(list_tile[:], source)
         nc.sync.dma_start(ga_sb[:], ga.rearrange("(p t) o -> p (t o)", t=PACK))
         nc.sync.dma_start(gb_sb[:], gb.rearrange("(p t) o -> p (t o)", t=PACK))
 
@@ -79,33 +101,31 @@ def tile_picked_selfratiosharewind_none_po_kernel(
         wds = sb.tile([P, H], U8, name="wds", align_bytes=64)
         nc.vector.tensor_copy(wd[:].rearrange("p (t m) -> p m t", t=PACK), ww[:].rearrange("p (m t) -> p m t", t=PACK))
         nc.vector.tensor_copy(xgs[:], xs[:].indirect(offs_sb[:]))
-        nc.vector.tensor_copy(wds[:].rearrange("p (t m) -> p m t", t=PACK), ws[:].rearrange("p (m t) -> p m t", t=PACK))
+        wds_by_tile = wds[:].rearrange("p (t m) -> p m t", t=PACK)
+        ws_by_tile = ws[:].rearrange("p (m t) -> p m t", t=PACK)
+        nc.vector.tensor_copy(wds_by_tile[:, :, 0], ws_by_tile[:, :, 0])
         for h in halves:
-            nc.vector.tensor_copy(xg[:, half(h)], xw[:].bitcast(U32).indirect(entries(offs_sb, h * W, W)))
+            nc.vector.tensor_copy(xg[:, half(h)], xw[:].bitcast(U32).indirect(entries(offs_sb, half(h))))
+        nc.vector.tensor_copy(wds_by_tile[:, :, 1:], ws_by_tile[:, :, 1:])
 
         ident = sb.tile([P, P], F32, name="ident", tag="ww")
         make_identity(nc, ident[:])
 
         def result_banks(name):
-            banks = [[(psum.tile([P, S], F32, name=f"{name}{t}", tag=f"a{t}"), slice(0, S))] for t in range(1, PACK)]
-            first = [(psum.tile([P, W], F32, name=f"{name}0_{h}", tag=f"{'ab'[h]}0"), half(h)) for h in halves]
-            return [first] + banks
+            whole = [[(psum.tile([P, S], F32, name=f"{name}{t}", tag=f"a{t}"), slice(0, S))] for t in range(1, PACK)]
+            halved = [(psum.tile([P, HALF], F32, name=f"{name}0_{h}", tag=f"{'ab'[h]}0"), half(h)) for h in halves]
+            return [halved] + whole
 
         y_ps = result_banks("y_ps")
         y = [sb.tile([P, S], F32, name=f"y{t}", tag=f"y{t}") for t in tiles]
         ex = [sb.tile([P, S], F32, name=f"ex{t}") for t in tiles]
-        e3 = [sb.tile([P, S], F32, name=f"e3_{t}") for t in tiles]
-        e4 = [sb.tile([P, S], F32, name=f"e4_{t}") for t in tiles]
-        pa = sb.tile([P, PACK * W], F32, name="pa")
-        pb = sb.tile([P, PACK * W], F32, name="pb")
-        rb = sb.tile([P, PACK * W], F32, name="rb")
+        ex3 = [sb.tile([P, S], F32, name=f"ex3_{t}") for t in tiles]
+        ex4 = {t: sb.tile([P, S], F32, name=f"ex4_{t}") for t in scalar_n4_tiles}
+        ex34 = {t: sb.tile([P, S], F32, name=f"ex34_{t}") for t in vector_n4_tiles}
+        pa = sb.tile([P, PACK * PAIRS], F32, name="pa")
+        pb = sb.tile([P, PACK * PAIRS], F32, name="pb")
+        rb = sb.tile([P, PACK * PAIRS], F32, name="rb")
         dt = [sb.tile([P, S], F32, name=f"dt{t}") for t in tiles]
-
-        def pairs(t):
-            return slice(t * W, (t + 1) * W)
-
-        def block(b):
-            return slice(b * P, (b + 1) * P)
 
         for t in tiles:
             for bank, cols in y_ps[t]:
@@ -122,134 +142,144 @@ def tile_picked_selfratiosharewind_none_po_kernel(
             for bank, cols in y_ps[t]:
                 nc.scalar.activation(ex[t][:, cols], bank[:], ACT.Exp, scale=0.5)
             for h in halves:
-                cols = slice(h * W, (h + 1) * W)
-                nc.scalar.activation(e3[t][:, cols], y[t][:].indirect(entries(n3_sb, h * W, W)), ACT.Exp, scale=0.5)
-            for h in halves:
-                cols = slice(h * W, (h + 1) * W)
-                if t < PACK - VECTOR_N4_TILES:
-                    nc.scalar.activation(e4[t][:, cols], y[t][:].indirect(entries(n4_sb, h * W, W)), ACT.Exp, scale=0.5)
+                nc.scalar.activation(ex3[t][:, half(h)], y[t][:].indirect(entries(n3_sb, half(h))), ACT.Exp, scale=0.5)
+            if t in scalar_n4_tiles:
+                for h in halves:
+                    nc.scalar.activation(
+                        ex4[t][:, half(h)], y[t][:].indirect(entries(n4_sb, half(h))), ACT.Exp, scale=0.5
+                    )
+        pb_size = sb.tile([P, PACK * PAIRS], F32, name="pb_size")
+        nc.scalar.activation(pb_size[:], pb[:], ACT.Abs)
 
-        nc.vector.tensor_tensor(rb[:], pa[:], pb[:], ALU.max)
+        for t in tiles:
+            nc.vector.tensor_tensor(rb[:, pairs(t)], pa[:, pairs(t)], pb[:, pairs(t)], ALU.max)
         for t in tiles:
             nc.vector.tensor_copy(dt[t][:].indirect(n2_sb[:]), rb[:, pairs(t)])
-        for t in range(PACK - VECTOR_N4_TILES, PACK):
+        for t in vector_n4_tiles:
             for h in halves:
                 nc.vector.tensor_tensor(
-                    e4[t][:, half(h)], ex[t][:].indirect(entries(n4_sb, h * W, W)), e3[t][:, half(h)], ALU.add
+                    ex34[t][:, half(h)], ex[t][:].indirect(entries(n4_sb, half(h))), ex3[t][:, half(h)], ALU.add
                 )
 
-        sum_ps = [psum.tile([P, S], F32, name=f"sum_ps{b}", tag=f"b{b}") for b in tiles]
+        sum_ps = [psum.tile([P, S], F32, name=f"sum_ps{t}", tag=f"b{t}") for t in tiles]
         for t in tiles:
-            terms = [ex[t], e4[t]] if t >= PACK - VECTOR_N4_TILES else [ex[t], e3[t], e4[t]]
-            for b in tiles:
+            terms = [ex[t], ex34[t]] if t in vector_n4_tiles else [ex[t], ex3[t], ex4[t]]
+            for b in blocks:
                 for i, term in enumerate(terms):
                     nc.tensor.matmul(
                         sum_ps[t][:, block(b)], term[:, block(b)], ident[:],
                         start=(i == 0), stop=(i == len(terms) - 1), is_transpose=True,
                     )
 
-        roots = sb.tile([P, PACK * (W + S)], F32, name="roots", tag=f"y{PACK - 1}")
-        den = sb.tile([P, PACK * W], F32, name="den")
-        inv = sb.tile([P, PACK * W], F32, name="inv")
+        roots = sb.tile([P, PACK * (PAIRS + S)], F32, name="roots", tag=f"y{PACK - 1}")
+        ra_factor = sb.tile([P, PACK * PAIRS], F32, name="ra_factor")
         for t in tiles:
-            nc.scalar.activation(roots[:, pairs(t)], pb[:, pairs(t)], ACT.Abs)
-            nc.scalar.activation(den[:, pairs(t)], roots[:, pairs(t)], ACT.Abs_reciprocal_sqrt, bias=0.5)
-            nc.scalar.activation(inv[:, pairs(t)], den[:, pairs(t)], ACT.Square)
-        root = [roots[:, PACK * W + t * S : PACK * W + (t + 1) * S] for t in tiles]
+            nc.scalar.activation(roots[:, pairs(t)], pb_size[:, pairs(t)], ACT.Abs_reciprocal_sqrt, bias=0.5)
+            nc.scalar.activation(ra_factor[:, pairs(t)], roots[:, pairs(t)], ACT.Square)
+        sum_root = [roots[:, PACK * PAIRS + t * S : PACK * PAIRS + (t + 1) * S] for t in tiles]
         back_ps = [psum.tile([P, S], F32, name=f"back_ps{t}", tag=f"a{t}") for t in tiles]
-        share = [sb.tile([P, S], F32, name=f"share{t}") for t in tiles]
-        zp = sb.tile([P, PACK, S], BF16, name="zp")
-        z2p = sb.tile([P, PACK, S], BF16, name="z2p")
+        two_over_sum = [sb.tile([P, S], F32, name=f"two_over_sum{t}") for t in tiles]
+        z_rows = sb.tile([P, PACK, S], BF16, name="z_rows")
+        z2_rows = sb.tile([P, PACK, S], BF16, name="z2_rows")
         for t in tiles:
-            nc.scalar.activation(root[t], sum_ps[t][:], ACT.Abs_reciprocal_sqrt, scale=0.5)
-            for b in tiles:
-                nc.tensor.transpose(back_ps[t][:, block(b)], root[t][:, block(b)], ident[:])
+            nc.scalar.activation(sum_root[t], sum_ps[t][:], ACT.Abs_reciprocal_sqrt, scale=0.5)
+            for b in blocks:
+                nc.tensor.transpose(back_ps[t][:, block(b)], sum_root[t][:, block(b)], ident[:])
         for t in tiles:
-            nc.scalar.activation(share[t][:], back_ps[t][:], ACT.Square)
+            nc.scalar.activation(two_over_sum[t][:], back_ps[t][:], ACT.Square)
 
-        def scatter_ra(t):
-            nc.vector.tensor_tensor(dt[t][:].indirect(n1_sb[:]), pa[:, pairs(t)], inv[:, pairs(t)], ALU.mult)
+        for t in tiles:
+            nc.vector.tensor_tensor(dt[t][:].indirect(n1_sb[:]), pa[:, pairs(t)], ra_factor[:, pairs(t)], ALU.mult)
             nc.scalar.activation(
-                zp[:, t, :].rearrange("p (u m) -> p m u", u=PACK), dt[t][:].rearrange("p (m u) -> p m u", u=PACK),
+                z_rows[:, t, :].rearrange("p (u m) -> p m u", u=PACK), dt[t][:].rearrange("p (m u) -> p m u", u=PACK),
                 ACT.Copy, scale=ga_sb[:, t : t + 1],
             )
-
-        for t in tiles:
-            scatter_ra(t)
-        for t in tiles:
-            nc.vector.scalar_tensor_tensor(z2p[:, t, :], share[t][:], gb_sb[:, t : t + 1], ex[t][:], ALU.mult, ALU.mult)
-
-        z2i = [sb.tile([P, W, PACK], BF16, name=f"z2i{h}", align_bytes=64) for h in halves]
-        z2c = sb.tile([P, S], U32, name="z2c", align_bytes=64)
-        z2s = sb.tile([P, S], U8, name="z2s", align_bytes=64)
-        for h in halves:
-            nc.vector.tensor_copy(
-                z2i[h][:].rearrange("p (c i) t -> p c t i", i=4), z2p[:, :, half(h)].rearrange("p t (c i) -> p c t i", i=4)
+        z2_pieces = [(t, slice(0, S)) for t in range(PACK - 1)] + [(PACK - 1, half(h)) for h in halves]
+        for t, cols in z2_pieces:
+            nc.vector.scalar_tensor_tensor(
+                z2_rows[:, t, cols], two_over_sum[t][:, cols], gb_sb[:, t : t + 1], ex[t][:, cols], ALU.mult, ALU.mult
             )
+
+        def regroup(copy, grouped, rows):
+            copy(grouped.rearrange("p (c i) t -> p c t i", i=RUN), rows.rearrange("p t (c i) -> p c t i", i=RUN))
+
+        z2_grouped = [sb.tile([P, HALF, PACK], BF16, name=f"z2_grouped{h}", align_bytes=64) for h in halves]
+        z2_codes = sb.tile([P, S], U32, name="z2_codes", align_bytes=64)
+        z2_scales = sb.tile([P, S], U8, name="z2_scales", align_bytes=64)
+        for h in halves:
+            regroup(nc.vector.tensor_copy, z2_grouped[h][:], z2_rows[:, :, half(h)])
         for h in halves:
             nc.vector.quantize_mx(
-                out=z2c[:, half(h)].bitcast(FP8X4), scales=z2s[:, half(h)], in_=z2i[h][:].rearrange("p j t -> p (j t)")
+                out=z2_codes[:, half(h)].bitcast(FP8X4), scales=z2_scales[:, half(h)],
+                in_=z2_grouped[h][:].rearrange("p j t -> p (j t)"),
             )
 
-        zi = [sb.tile([P, P, PACK], BF16, name=f"zi{u}", align_bytes=64) for u in tiles]
-        zc = [sb.tile([P, P], U32, name=f"zc{u}", align_bytes=64) for u in tiles]
-        zs = [sb.tile([P, P], U8, name=f"zs{u}", align_bytes=64) for u in tiles]
+        z_grouped = [sb.tile([P, P, PACK], BF16, name=f"z_grouped{u}", align_bytes=64) for u in tiles]
+        z_codes = [sb.tile([P, P], U32, name=f"z_codes{u}", align_bytes=64) for u in tiles]
+        z_scales = [sb.tile([P, P], U8, name=f"z_scales{u}", align_bytes=64) for u in tiles]
         s_ps = result_banks("s_ps")
         s = [sb.tile([P, S], F32, name=f"s{u}") for u in tiles]
         for u in tiles:
-            nc.scalar.copy(
-                zi[u][:].rearrange("p (c i) t -> p c t i", i=4), zp[:, :, block(u)].rearrange("p t (c i) -> p c t i", i=4)
+            regroup(nc.scalar.copy, z_grouped[u][:], z_rows[:, :, block(u)])
+            nc.vector.quantize_mx(
+                out=z_codes[u][:].bitcast(FP8X4), scales=z_scales[u][:], in_=z_grouped[u][:].rearrange("p m t -> p (m t)")
             )
-            nc.vector.quantize_mx(out=zc[u][:].bitcast(FP8X4), scales=zs[u][:], in_=zi[u][:].rearrange("p m t -> p (m t)"))
             for bank, cols in s_ps[u]:
                 nc.tensor.matmul_mx(
-                    out=bank[:], lhsT=zc[u][:].bitcast(FP8X4), lhsT_scale=zs[u][:],
-                    rhs=z2c[:, cols].bitcast(FP8X4), rhs_scale=z2s[:, cols], start=True, stop=True,
+                    out=bank[:], lhsT=z_codes[u][:].bitcast(FP8X4), lhsT_scale=z_scales[u][:],
+                    rhs=z2_codes[:, cols].bitcast(FP8X4), rhs_scale=z2_scales[:, cols], start=True, stop=True,
                 )
                 nc.scalar.activation(s[u][:, cols], bank[:], ACT.Copy, scale=0.0625)
 
         out_rows = out_0.rearrange("(p u) j -> p u j", u=PACK)
-        out_words = out_1[0].rearrange("p n t -> p (n t)").bitcast(I32)
-        oc = sb.tile([P, S], I32, name="oc", align_bytes=64)
-        osc = sb.tile([P, S], U8, name="osc", align_bytes=64)
-        chunks = range(S // P)
-        last = PACK - 1
-        o = sb.tile([P, S // P, PACK, P], F32, name="o")
-        for u in range(last):
-            g6 = sb.tile([P, S], F32, name=f"g6_{u}")
-            d = sb.tile([P, S], F32, name=f"d_{u}")
+        out_words = words_of(out_1)
+        out_codes = sb.tile([P, S], I32, name="out_codes", align_bytes=64)
+        out_scales = sb.tile([P, S], U8, name="out_scales", align_bytes=64)
+        result = sb.tile([P, S // P, PACK, P], F32, name="result")
+        chunks_in_half = HALF // P
+        for u in range(WHOLE_TILES):
+            s6 = sb.tile([P, S], F32, name=f"s6_{u}")
+            diff = sb.tile([P, S], F32, name=f"diff_{u}")
             for h in halves:
-                nc.vector.tensor_copy(g6[:, half(h)], s[u][:].indirect(entries(n6_sb, h * W, W)))
-            for h in halves:
-                nc.vector.tensor_tensor(d[:, half(h)], s[u][:].indirect(entries(n5_sb, h * W, W)), g6[:, half(h)], ALU.subtract)
+                nc.vector.tensor_copy(s6[:, half(h)], s[u][:].indirect(entries(n6_sb, half(h))))
             for h in halves:
                 nc.vector.tensor_tensor(
-                    o[:, 2 * h : 2 * h + 2, u, :], d[:, half(h)].rearrange("p (c j) -> p c j", j=P),
+                    diff[:, half(h)], s[u][:].indirect(entries(n5_sb, half(h))), s6[:, half(h)], ALU.subtract
+                )
+            for h in halves:
+                nc.vector.tensor_tensor(
+                    result[:, chunks_in_half * h : chunks_in_half * (h + 1), u, :],
+                    diff[:, half(h)].rearrange("p (c j) -> p c j", j=P),
                     s[u][:, half(h)].rearrange("p (c j) -> p c j", j=P), ALU.mult,
                 )
-            nc.sync.dma_start(out_rows[:, u, :].rearrange("p (c j) -> p c j", j=P), o[:, :, u, :])
-        g6 = sb.tile([P, S], F32, name="g6_last")
-        d = sb.tile([P, S], F32, name="d_last")
-        for h in halves:
-            nc.vector.tensor_copy(g6[:, half(h)], s[last][:].indirect(entries(n6_sb, h * W, W)))
-        for c in range(len(chunks) + 1):
-            if c < len(chunks):
-                nc.vector.tensor_tensor(d[:, block(c)], s[last][:].indirect(entries(n5_sb, c * P, P)), g6[:, block(c)], ALU.subtract)
-            if c > 0:
-                nc.vector.tensor_tensor(o[:, c - 1, last, :], d[:, block(c - 1)], s[last][:, block(c - 1)], ALU.mult)
-        for c in chunks:
-            ob = sb.tile([P, P, PACK], BF16, name=f"ob{c}", align_bytes=64)
-            nc.scalar.copy(ob[:], o[:, c].rearrange("p u j -> p j u"))
-            nc.vector.quantize_mx(
-                out=oc[:, block(c)].bitcast(FP8X4), scales=osc[:, block(c)], in_=ob[:].rearrange("p j u -> p (j u)")
-            )
-        for h in halves:
-            nc.sync.dma_start(
-                out_rows[:, last, half(h)].rearrange("p (c j) -> p c j", j=P), o[:, 2 * h : 2 * h + 2, last, :]
-            )
-        early = slice(0, S - P)
-        nc.sync.dma_start(out_words[:, early], oc[:, early])
-        nc.sync.dma_start(out_words[:, block(chunks[-1])], oc[:, block(chunks[-1])])
-        for q in range(4):
-            eng = nc.sync if q % 2 == 0 else nc.scalar
-            eng.dma_start(out_2[0][4 * q : 4 * q + 4, :].bitcast(I32), osc[32 * q : 32 * q + 4, :].bitcast(I32))
+            nc.sync.dma_start(out_rows[:, u, :].rearrange("p (c j) -> p c j", j=P), result[:, :, u, :])
+
+        late_tiles = range(WHOLE_TILES, PACK)
+        last_chunk = blocks[-1]
+        for c in blocks:
+            s6 = sb.tile([P, len(late_tiles), P], F32, name=f"s6_late{c}", tag="s6_late")
+            diff = sb.tile([P, len(late_tiles), P], F32, name=f"diff_late{c}")
+            for i, u in enumerate(late_tiles):
+                nc.vector.tensor_copy(s6[:, i, :], s[u][:].indirect(entries(n6_sb, block(c))))
+            for i, u in enumerate(late_tiles):
+                nc.vector.tensor_tensor(
+                    diff[:, i, :], s[u][:].indirect(entries(n5_sb, block(c))), s6[:, i, :], ALU.subtract
+                )
+            for i, u in enumerate(late_tiles):
+                nc.vector.tensor_tensor(result[:, c, u, :], diff[:, i, :], s[u][:, block(c)], ALU.mult)
+            nc.sync.dma_start(out_rows[:, WHOLE_TILES:, block(c)], result[:, c, WHOLE_TILES:, :])
+            copies = [nc.scalar.copy, nc.vector.tensor_copy] if c == last_chunk else [nc.scalar.copy]
+            width = P // len(copies)
+            for i, copy in enumerate(copies):
+                grouped = sb.tile([P, width, PACK], BF16, name=f"out_grouped{c}_{i}", align_bytes=64)
+                cols = slice(c * P + i * width, c * P + (i + 1) * width)
+                copy(grouped[:], result[:, c, :, i * width : (i + 1) * width].rearrange("p u j -> p j u"))
+                nc.vector.quantize_mx(
+                    out=out_codes[:, cols].bitcast(FP8X4), scales=out_scales[:, cols],
+                    in_=grouped[:].rearrange("p j u -> p (j u)"),
+                )
+        for cols in (slice(0, last_chunk * P), block(last_chunk)):
+            nc.sync.dma_start(out_words[:, cols], out_codes[:, cols])
+        for q in range(QUADRANTS):
+            queue = nc.sync if q % 2 == 0 else nc.scalar
+            queue.dma_start(scale_rows_in_hbm(out_2, q), scale_rows_in_sbuf(out_scales, q))

from contextlib import ExitStack

import concourse.mybir as mybir
from concourse.masks import make_identity

F32 = mybir.dt.float32
BF16 = mybir.dt.bfloat16
I32 = mybir.dt.int32
U32 = mybir.dt.uint32
U16 = mybir.dt.uint16
U8 = mybir.dt.uint8
FP8X4 = mybir.dt.float8_e4m3fn_x4
ACT = mybir.ActivationFunctionType
ALU = mybir.AluOpType

P = 128
PACK = 4
QUADRANTS = 4
LIST_ROWS = 16
K, T, S, H = 512, 2048, 512, 512
PAIRS = 256
HALF = S // 2
RUN = 4
FLOPS = 2 * K * H * S + 2 * H * S * S

VECTOR_N4_TILES = 2
WHOLE_TILES = 2
GPSIMD_SCALE_LOADS = 2


def tile_picked_selfratiosharewind_none_po_kernel(
    tc, x_words, x_scales, w1_words, w1_scales, ga, gb, offs, n1, n2, n3, n4, n5, n6, out_0, out_1, out_2
):
    nc = tc.nc
    tiles = range(PACK)
    halves = range(S // HALF)
    blocks = range(S // P)
    scalar_n4_tiles = range(PACK - VECTOR_N4_TILES)
    vector_n4_tiles = range(PACK - VECTOR_N4_TILES, PACK)

    def half(h):
        return slice(h * HALF, (h + 1) * HALF)

    def block(b):
        return slice(b * P, (b + 1) * P)

    def pairs(t):
        return slice(t * PAIRS, (t + 1) * PAIRS)

    def entries(list_tile, cols):
        return list_tile[:, cols.start // LIST_ROWS : cols.stop // LIST_ROWS]

    def words_of(packed):
        return packed[0].rearrange("p n t -> p (n t)").bitcast(I32)

    def scale_rows_in_hbm(rows, q):
        return rows[0][4 * q : 4 * q + 4, :].bitcast(I32)

    def scale_rows_in_sbuf(scale_tile, q):
        return scale_tile[32 * q : 32 * q + 4, :].bitcast(I32)

    with ExitStack() as ctx:
        lists = ctx.enter_context(tc.tile_pool(name="lists", bufs=1))
        sb = ctx.enter_context(tc.tile_pool(name="sb", bufs=1))
        psum = ctx.enter_context(tc.psum_pool(name="psum", bufs=1))

        offs_sb = lists.tile(list(offs.shape), U16, name="offs_sb")
        n1_sb = lists.tile(list(n1.shape), U16, name="n1_sb")
        n2_sb = lists.tile(list(n2.shape), U16, name="n2_sb")
        n3_sb = lists.tile(list(n3.shape), U16, name="n3_sb")
        n4_sb = lists.tile(list(n4.shape), U16, name="n4_sb")
        n5_sb = lists.tile(list(n5.shape), U16, name="n5_sb")
        n6_sb = lists.tile(list(n6.shape), U16, name="n6_sb")

        xw = sb.tile([P, T], I32, name="xw")
        xs = sb.tile([P, T], U8, name="xs")
        ww = sb.tile([P, H], I32, name="ww", tag="ww")
        ws = sb.tile([P, H], U8, name="ws")
        ga_sb = sb.tile([P, PACK], F32, name="ga_sb")
        gb_sb = sb.tile([P, PACK], F32, name="gb_sb")

        nc.gpsimd.memset(ws[:].bitcast(I32), 0)
        nc.vector.memset(xs[:].bitcast(I32), 0)
        nc.sync.dma_start(offs_sb[:], offs)
        nc.sync.dma_start(ww[:], words_of(w1_words))
        for q in range(QUADRANTS):
            nc.sync.dma_start(scale_rows_in_sbuf(xs, q), scale_rows_in_hbm(x_scales, q))
        for q in range(QUADRANTS - 1):
            queue = nc.gpsimd if q < GPSIMD_SCALE_LOADS else nc.sync
            queue.dma_start(scale_rows_in_sbuf(ws, q), scale_rows_in_hbm(w1_scales, q))
        nc.sync.dma_start(xw[:], words_of(x_words))
        nc.sync.dma_start(scale_rows_in_sbuf(ws, QUADRANTS - 1), scale_rows_in_hbm(w1_scales, QUADRANTS - 1))
        for list_tile, source in ((n1_sb, n1), (n2_sb, n2), (n3_sb, n3), (n4_sb, n4), (n5_sb, n5), (n6_sb, n6)):
            nc.sync.dma_start(list_tile[:], source)
        nc.sync.dma_start(ga_sb[:], ga.rearrange("(p t) o -> p (t o)", t=PACK))
        nc.sync.dma_start(gb_sb[:], gb.rearrange("(p t) o -> p (t o)", t=PACK))

        xg = sb.tile([P, S], U32, name="xg", align_bytes=64)
        xgs = sb.tile([P, S], U8, name="xgs", align_bytes=64)
        wd = sb.tile([P, H], I32, name="wd", align_bytes=64)
        wds = sb.tile([P, H], U8, name="wds", align_bytes=64)
        nc.vector.tensor_copy(wd[:].rearrange("p (t m) -> p m t", t=PACK), ww[:].rearrange("p (m t) -> p m t", t=PACK))
        nc.vector.tensor_copy(xgs[:], xs[:].indirect(offs_sb[:]))
        wds_by_tile = wds[:].rearrange("p (t m) -> p m t", t=PACK)
        ws_by_tile = ws[:].rearrange("p (m t) -> p m t", t=PACK)
        nc.vector.tensor_copy(wds_by_tile[:, :, 0], ws_by_tile[:, :, 0])
        for h in halves:
            nc.vector.tensor_copy(xg[:, half(h)], xw[:].bitcast(U32).indirect(entries(offs_sb, half(h))))
        nc.vector.tensor_copy(wds_by_tile[:, :, 1:], ws_by_tile[:, :, 1:])

        ident = sb.tile([P, P], F32, name="ident", tag="ww")
        make_identity(nc, ident[:])

        def result_banks(name):
            whole = [[(psum.tile([P, S], F32, name=f"{name}{t}", tag=f"a{t}"), slice(0, S))] for t in range(1, PACK)]
            halved = [(psum.tile([P, HALF], F32, name=f"{name}0_{h}", tag=f"{'ab'[h]}0"), half(h)) for h in halves]
            return [halved] + whole

        y_ps = result_banks("y_ps")
        y = [sb.tile([P, S], F32, name=f"y{t}", tag=f"y{t}") for t in tiles]
        ex = [sb.tile([P, S], F32, name=f"ex{t}") for t in tiles]
        ex3 = [sb.tile([P, S], F32, name=f"ex3_{t}") for t in tiles]
        ex4 = {t: sb.tile([P, S], F32, name=f"ex4_{t}") for t in scalar_n4_tiles}
        ex34 = {t: sb.tile([P, S], F32, name=f"ex34_{t}") for t in vector_n4_tiles}
        pa = sb.tile([P, PACK * PAIRS], F32, name="pa")
        pb = sb.tile([P, PACK * PAIRS], F32, name="pb")
        rb = sb.tile([P, PACK * PAIRS], F32, name="rb")
        dt = [sb.tile([P, S], F32, name=f"dt{t}") for t in tiles]

        for t in tiles:
            for bank, cols in y_ps[t]:
                nc.tensor.matmul_mx(
                    out=bank[:], lhsT=wd[:, block(t)].bitcast(FP8X4), lhsT_scale=wds[:, block(t)],
                    rhs=xg[:, cols].bitcast(FP8X4), rhs_scale=xgs[:, cols], start=True, stop=True,
                )
                nc.scalar.copy(y[t][:, cols], bank[:])
        for t in tiles:
            nc.vector.tensor_copy(pa[:, pairs(t)], y[t][:].indirect(n1_sb[:]))
            nc.vector.tensor_copy(pb[:, pairs(t)], y[t][:].indirect(n2_sb[:]))

        for t in tiles:
            for bank, cols in y_ps[t]:
                nc.scalar.activation(ex[t][:, cols], bank[:], ACT.Exp, scale=0.5)
            for h in halves:
                nc.scalar.activation(ex3[t][:, half(h)], y[t][:].indirect(entries(n3_sb, half(h))), ACT.Exp, scale=0.5)
            if t in scalar_n4_tiles:
                for h in halves:
                    nc.scalar.activation(
                        ex4[t][:, half(h)], y[t][:].indirect(entries(n4_sb, half(h))), ACT.Exp, scale=0.5
                    )
        pb_size = sb.tile([P, PACK * PAIRS], F32, name="pb_size")
        nc.scalar.activation(pb_size[:], pb[:], ACT.Abs)

        for t in tiles:
            nc.vector.tensor_tensor(rb[:, pairs(t)], pa[:, pairs(t)], pb[:, pairs(t)], ALU.max)
        for t in tiles:
            nc.vector.tensor_copy(dt[t][:].indirect(n2_sb[:]), rb[:, pairs(t)])
        for t in vector_n4_tiles:
            for h in halves:
                nc.vector.tensor_tensor(
                    ex34[t][:, half(h)], ex[t][:].indirect(entries(n4_sb, half(h))), ex3[t][:, half(h)], ALU.add
                )

        sum_ps = [psum.tile([P, S], F32, name=f"sum_ps{t}", tag=f"b{t}") for t in tiles]
        for t in tiles:
            terms = [ex[t], ex34[t]] if t in vector_n4_tiles else [ex[t], ex3[t], ex4[t]]
            for b in blocks:
                for i, term in enumerate(terms):
                    nc.tensor.matmul(
                        sum_ps[t][:, block(b)], term[:, block(b)], ident[:],
                        start=(i == 0), stop=(i == len(terms) - 1), is_transpose=True,
                    )

        roots = sb.tile([P, PACK * (PAIRS + S)], F32, name="roots", tag=f"y{PACK - 1}")
        ra_factor = sb.tile([P, PACK * PAIRS], F32, name="ra_factor")
        for t in tiles:
            nc.scalar.activation(roots[:, pairs(t)], pb_size[:, pairs(t)], ACT.Abs_reciprocal_sqrt, bias=0.5)
            nc.scalar.activation(ra_factor[:, pairs(t)], roots[:, pairs(t)], ACT.Square)
        sum_root = [roots[:, PACK * PAIRS + t * S : PACK * PAIRS + (t + 1) * S] for t in tiles]
        back_ps = [psum.tile([P, S], F32, name=f"back_ps{t}", tag=f"a{t}") for t in tiles]
        two_over_sum = [sb.tile([P, S], F32, name=f"two_over_sum{t}") for t in tiles]
        z_rows = sb.tile([P, PACK, S], BF16, name="z_rows")
        z2_rows = sb.tile([P, PACK, S], BF16, name="z2_rows")
        for t in tiles:
            nc.scalar.activation(sum_root[t], sum_ps[t][:], ACT.Abs_reciprocal_sqrt, scale=0.5)
            for b in blocks:
                nc.tensor.transpose(back_ps[t][:, block(b)], sum_root[t][:, block(b)], ident[:])
        for t in tiles:
            nc.scalar.activation(two_over_sum[t][:], back_ps[t][:], ACT.Square)

        for t in tiles:
            nc.vector.tensor_tensor(dt[t][:].indirect(n1_sb[:]), pa[:, pairs(t)], ra_factor[:, pairs(t)], ALU.mult)
            nc.scalar.activation(
                z_rows[:, t, :].rearrange("p (u m) -> p m u", u=PACK), dt[t][:].rearrange("p (m u) -> p m u", u=PACK),
                ACT.Copy, scale=ga_sb[:, t : t + 1],
            )
        z2_pieces = [(t, slice(0, S)) for t in range(PACK - 1)] + [(PACK - 1, half(h)) for h in halves]
        for t, cols in z2_pieces:
            nc.vector.scalar_tensor_tensor(
                z2_rows[:, t, cols], two_over_sum[t][:, cols], gb_sb[:, t : t + 1], ex[t][:, cols], ALU.mult, ALU.mult
            )

        def regroup(copy, grouped, rows):
            copy(grouped.rearrange("p (c i) t -> p c t i", i=RUN), rows.rearrange("p t (c i) -> p c t i", i=RUN))

        z2_grouped = [sb.tile([P, HALF, PACK], BF16, name=f"z2_grouped{h}", align_bytes=64) for h in halves]
        z2_codes = sb.tile([P, S], U32, name="z2_codes", align_bytes=64)
        z2_scales = sb.tile([P, S], U8, name="z2_scales", align_bytes=64)
        for h in halves:
            regroup(nc.vector.tensor_copy, z2_grouped[h][:], z2_rows[:, :, half(h)])
        for h in halves:
            nc.vector.quantize_mx(
                out=z2_codes[:, half(h)].bitcast(FP8X4), scales=z2_scales[:, half(h)],
                in_=z2_grouped[h][:].rearrange("p j t -> p (j t)"),
            )

        z_grouped = [sb.tile([P, P, PACK], BF16, name=f"z_grouped{u}", align_bytes=64) for u in tiles]
        z_codes = [sb.tile([P, P], U32, name=f"z_codes{u}", align_bytes=64) for u in tiles]
        z_scales = [sb.tile([P, P], U8, name=f"z_scales{u}", align_bytes=64) for u in tiles]
        s_ps = result_banks("s_ps")
        s = [sb.tile([P, S], F32, name=f"s{u}") for u in tiles]
        for u in tiles:
            regroup(nc.scalar.copy, z_grouped[u][:], z_rows[:, :, block(u)])
            nc.vector.quantize_mx(
                out=z_codes[u][:].bitcast(FP8X4), scales=z_scales[u][:], in_=z_grouped[u][:].rearrange("p m t -> p (m t)")
            )
            for bank, cols in s_ps[u]:
                nc.tensor.matmul_mx(
                    out=bank[:], lhsT=z_codes[u][:].bitcast(FP8X4), lhsT_scale=z_scales[u][:],
                    rhs=z2_codes[:, cols].bitcast(FP8X4), rhs_scale=z2_scales[:, cols], start=True, stop=True,
                )
                nc.scalar.activation(s[u][:, cols], bank[:], ACT.Copy, scale=0.0625)

        out_rows = out_0.rearrange("(p u) j -> p u j", u=PACK)
        out_words = words_of(out_1)
        out_codes = sb.tile([P, S], I32, name="out_codes", align_bytes=64)
        out_scales = sb.tile([P, S], U8, name="out_scales", align_bytes=64)
        result = sb.tile([P, S // P, PACK, P], F32, name="result")
        chunks_in_half = HALF // P
        for u in range(WHOLE_TILES):
            s6 = sb.tile([P, S], F32, name=f"s6_{u}")
            diff = sb.tile([P, S], F32, name=f"diff_{u}")
            for h in halves:
                nc.vector.tensor_copy(s6[:, half(h)], s[u][:].indirect(entries(n6_sb, half(h))))
            for h in halves:
                nc.vector.tensor_tensor(
                    diff[:, half(h)], s[u][:].indirect(entries(n5_sb, half(h))), s6[:, half(h)], ALU.subtract
                )
            for h in halves:
                nc.vector.tensor_tensor(
                    result[:, chunks_in_half * h : chunks_in_half * (h + 1), u, :],
                    diff[:, half(h)].rearrange("p (c j) -> p c j", j=P),
                    s[u][:, half(h)].rearrange("p (c j) -> p c j", j=P), ALU.mult,
                )
            nc.sync.dma_start(out_rows[:, u, :].rearrange("p (c j) -> p c j", j=P), result[:, :, u, :])

        late_tiles = range(WHOLE_TILES, PACK)
        last_chunk = blocks[-1]
        for c in blocks:
            s6 = sb.tile([P, len(late_tiles), P], F32, name=f"s6_late{c}", tag="s6_late")
            diff = sb.tile([P, len(late_tiles), P], F32, name=f"diff_late{c}")
            for i, u in enumerate(late_tiles):
                nc.vector.tensor_copy(s6[:, i, :], s[u][:].indirect(entries(n6_sb, block(c))))
            for i, u in enumerate(late_tiles):
                nc.vector.tensor_tensor(
                    diff[:, i, :], s[u][:].indirect(entries(n5_sb, block(c))), s6[:, i, :], ALU.subtract
                )
            for i, u in enumerate(late_tiles):
                nc.vector.tensor_tensor(result[:, c, u, :], diff[:, i, :], s[u][:, block(c)], ALU.mult)
            nc.sync.dma_start(out_rows[:, WHOLE_TILES:, block(c)], result[:, c, WHOLE_TILES:, :])
            copies = [nc.scalar.copy, nc.vector.tensor_copy] if c == last_chunk else [nc.scalar.copy]
            width = P // len(copies)
            for i, copy in enumerate(copies):
                grouped = sb.tile([P, width, PACK], BF16, name=f"out_grouped{c}_{i}", align_bytes=64)
                cols = slice(c * P + i * width, c * P + (i + 1) * width)
                copy(grouped[:], result[:, c, :, i * width : (i + 1) * width].rearrange("p u j -> p j u"))
                nc.vector.quantize_mx(
                    out=out_codes[:, cols].bitcast(FP8X4), scales=out_scales[:, cols],
                    in_=grouped[:].rearrange("p j u -> p (j u)"),
                )
        for cols in (slice(0, last_chunk * P), block(last_chunk)):
            nc.sync.dma_start(out_words[:, cols], out_codes[:, cols])
        for q in range(QUADRANTS):
            queue = nc.sync if q % 2 == 0 else nc.scalar
            queue.dma_start(scale_rows_in_hbm(out_2, q), scale_rows_in_sbuf(out_scales, q))
